import numpy as np
import ml_dtypes


def mxq(x, axis, fmt="e4m3"):
    dtype, down = {"e4m3": (ml_dtypes.float8_e4m3fn, 7), "e5m2": (ml_dtypes.float8_e5m2, 14)}[fmt]
    v = np.moveaxis(np.asarray(x, np.float32).astype(ml_dtypes.bfloat16).astype(np.float64), axis, -1)
    blocks = v.reshape(v.shape[:-1] + (-1, 32))
    amax = np.abs(blocks).max(-1, keepdims=True)
    byte = np.maximum(np.where(amax > 0, np.frexp(amax)[1] - 1 + 127, 0) - down, 1)
    scale = np.exp2(byte - 127.0)
    codes = (blocks / scale).astype(np.float32).astype(dtype).astype(np.float64)
    return np.moveaxis((codes * scale).reshape(v.shape), -1, axis)


WIDE = False


def mx_kscale(k):
    if not WIDE:
        return np.ones(k)
    levels = np.array([10, -10, 5, -5, 0])
    if k % 512:
        return np.exp2(np.random.permutation(np.resize(levels, k // 32))).repeat(32)
    a = np.empty((k // 512, 16))
    for p in range(k // 512):
        a[p, :8] = np.random.permutation(np.resize(levels, 8))
        for g in range(8):
            far = levels[np.abs(levels - a[p, g]) >= 10]
            a[p, g + 8] = far[np.random.randint(len(far))]
    return np.exp2(a.ravel()).repeat(32)


def f64(x):
    return np.asarray(x).astype(np.float64)


def striped(idx):
    return np.tile(np.asarray(idx).reshape(-1, 16).T, (8, 1)).astype(np.uint16)


def unstriped(offs):
    return offs[:16].T.reshape(-1).astype(np.int64)


def striped8(idx):
    return np.asarray(idx).reshape(8, -1, 16).transpose(0, 2, 1).reshape(128, -1).astype(np.uint16)


def unstriped8(offs):
    return offs.reshape(8, 16, -1).transpose(0, 2, 1).reshape(8, -1).astype(np.int64)


def pick8(x, idx, run):
    r = np.arange(len(x))
    return x[r[:, None], idx[r % (8 * run) // run]]


E2M1 = np.array([0.0, 0.5, 1.0, 1.5, 2.0, 3.0, 4.0, 6.0, -0.0, -0.5, -1.0, -1.5, -2.0, -3.0, -4.0, -6.0])


def pack_weight(w, fmt):
    k, n = w.shape
    w = f64(np.asarray(w, np.float32).astype(ml_dtypes.bfloat16)).reshape(k // 32, 32, n)
    amax = np.abs(w).max(1)
    if fmt == "e4m3":
        byte = np.frexp(amax)[1] - 1 + 127 - 7
    else:
        mant, ex = np.frexp(amax / 6.0)
        byte = np.where(mant > 0.5, ex, ex - 1) + 127
    byte = np.clip(np.where(amax > 0, byte, 1), 1, 254)
    scaled = (w * np.exp2(127.0 - byte)[:, None, :]).reshape(k, n).astype(np.float32)
    by_word = np.ascontiguousarray(scaled.reshape(k // 512, 128, 4, n).transpose(0, 1, 3, 2))
    if fmt == "e4m3":
        words = by_word.astype(ml_dtypes.float8_e4m3fn).view(np.uint8)
    else:
        c = by_word.astype(ml_dtypes.float4_e2m1fn).view(np.uint8) & 0xF
        words = (c[..., 0::2] | (c[..., 1::2] << 4)).reshape(k // 512, 128, 2 * n)
    return np.ascontiguousarray(words), np.ascontiguousarray(byte.astype(np.uint8).reshape(k // 512, 16, n))


def unpack_weight(words, scales, fmt):
    g, _, n = scales.shape
    words = np.ascontiguousarray(words).reshape(g, 128, n, -1)
    if fmt == "e4m3":
        vals = words.view(ml_dtypes.float8_e4m3fn).astype(np.float64)
    else:
        nib = np.empty((g, 128, n, 4), np.uint8)
        nib[..., 0::2] = words & 0xF
        nib[..., 1::2] = words >> 4
        vals = E2M1[nib]
    vals = vals * np.repeat(np.exp2(scales.astype(np.float64) - 127.0), 8, axis=1)[..., None]
    return vals.transpose(0, 1, 3, 2).reshape(g * 512, n)


def sgn(shape):
    return np.random.uniform(0.5, 2.0, shape) * np.where(np.random.standard_normal(shape) < 0, -1.0, 1.0)


K, J, R, T, Z, M, O, N, U, E = 512, 512, 512, 1024, 512, 1024, 256, 256, 128, 512


def setup_inputs():
    n = np.random.standard_normal
    idx = np.stack([np.random.permutation(T)[:J] for _ in range(8)])
    idx2 = np.stack([np.random.permutation(T)[:J] for _ in range(8)])
    idx3 = np.random.permutation(M)[:J]
    idx4 = np.stack([np.random.permutation(J)[:O] for _ in range(8)])
    idx5 = np.stack([np.random.permutation(J)[:O] for _ in range(8)])
    idx6 = np.stack([np.random.permutation(O)[:U] for _ in range(8)])
    idx7 = np.stack([np.random.permutation(E)[:U] for _ in range(8)])
    fk = mx_kscale(K)
    fr = mx_kscale(R)
    fz = mx_kscale(Z)
    wp = pack_weight(n((K, R)) * 1 / np.sqrt(K) / fk[:, None] * fr, "e2m1")
    xop = pack_weight(n((Z, M)) / fz[:, None], "e2m1")
    w2p = pack_weight(n((Z, R)) * 1 / np.sqrt(Z) * fz[:, None] * fr, "e4m3")
    wbp = pack_weight(n((R, N)) * 1 / np.sqrt(R) / fr[:, None], "e4m3")
    return {
        "ta": (np.random.randint(-7, 8, (K, T)).astype(np.float64)).astype(np.float32),
        "ga": ((np.random.randint(10, 25, (K, 1)) / 64.0) * fk[:, None]).astype(np.float32),
        "gb": ((np.random.randint(4, 13, (K, 1)) / 64.0) * fk[:, None]).astype(np.float32),
        "w_words": wp[0],
        "w_scales": wp[1],
        "xo_words": xop[0],
        "xo_scales": xop[1],
        "w2_words": w2p[0],
        "w2_scales": w2p[1],
        "sa": (np.random.uniform(0.5, 1.6, (R, 1))).astype(np.float32),
        "sb": (np.random.uniform(0.5, 1.6, (R, 1))).astype(np.float32),
        "wb_words": wbp[0],
        "wb_scales": wbp[1],
        "so": (sgn((N, 1))).astype(np.float32),
        "offs": striped8(idx),
        "offs2": striped8(idx2),
        "offs3": striped(idx3),
        "offs4": striped8(idx4),
        "offs5": striped8(idx5),
        "offs6": striped8(idx6),
        "offs7": striped8(idx7),
    }


def reference(ta, ga, gb, w_words, w_scales, xo_words, xo_scales, w2_words, w2_scales, sa, sb, wb_words, wb_scales, so, offs, offs2, offs3, offs4, offs5, offs6, offs7):
    idx = unstriped8(offs)
    idx2 = unstriped8(offs2)
    idx3 = unstriped(offs3)
    idx4 = unstriped8(offs4)
    idx5 = unstriped8(offs5)
    idx6 = unstriped8(offs6)
    idx7 = unstriped8(offs7)
    wu = unpack_weight(w_words, w_scales, "e2m1")
    xou = unpack_weight(xo_words, xo_scales, "e2m1")
    w2u = unpack_weight(w2_words, w2_scales, "e4m3")
    wbu = unpack_weight(wb_words, wb_scales, "e4m3")
    xc = pick8(f64(ta), idx, 64) * f64(ga) + pick8(f64(ta), idx2, 64) * f64(gb)
    xcq = mxq(xc, 0, "e4m3")
    a = wu.T @ xcq
    xoidx3g = xou[:, idx3]
    b = w2u.T @ xoidx3g
    hid = np.maximum(pick8(a, idx4, 64) * f64(sa), pick8(b, idx5, 64) * f64(sb))
    hidq = mxq(hid, 0, "e4m3")
    p = wbu.T @ hidq
    m0 = pick8(p, idx6, 16) * f64(so)
    y = np.zeros((N, E))
    y[np.arange(N)[:, None], idx7[np.arange(N) % 128 // 16]] = m0
    return y

@@ -1,0 +1,229 @@
+from contextlib import ExitStack
+
+import concourse.mybir as mybir
+
+K, J, R, T, Z, M, O, N, U, E = 512, 512, 512, 1024, 512, 1024, 256, 256, 128, 512
+FLOPS = 2 * (K * R * J + Z * R * J + R * N * O)
+
+F32 = mybir.dt.float32
+BF16 = mybir.dt.bfloat16
+I32 = mybir.dt.int32
+U32 = mybir.dt.uint32
+U16 = mybir.dt.uint16
+U8 = mybir.dt.uint8
+FP8X4 = mybir.dt.float8_e4m3fn_x4
+FP4X4 = mybir.dt.float4_e2m1fn_x4
+COPY = mybir.ActivationFunctionType.Copy
+ADD = mybir.AluOpType.add
+MAX = mybir.AluOpType.max
+
+P = 128
+PACK = 4
+LIST_ROWS = 16
+JH = J // 2
+OH = O // 2
+
+
+def tile_picked_refined_plain_two_groupmeet_one_posted_kernel(
+    tc, ta, ga, gb, w_words, w_scales, xo_words, xo_scales, w2_words, w2_scales, sa, sb,
+    wb_words, wb_scales, so, offs, offs2, offs3, offs4, offs5, offs6, offs7, out,
+):
+    nc = tc.nc
+    with ExitStack() as ctx:
+        keep = ctx.enter_context(tc.tile_pool(name="keep", bufs=1))
+        psum = ctx.enter_context(tc.psum_pool(name="psum", bufs=1))
+
+        def sb_tile(shape, dtype, name, tag=None):
+            return keep.tile(shape, dtype, name=name, tag=tag or name, align_bytes=64)
+
+        def load_list(src, name):
+            tile = sb_tile(list(src.shape), U16, name)
+            nc.sync.dma_start(tile[:], src)
+            return tile
+
+        def load_rowvec(src, name):
+            tile = sb_tile([P, PACK], F32, name)
+            nc.sync.dma_start(tile[:], src.rearrange("(p t) o -> p (t o)", t=PACK))
+            return tile
+
+        def zeroed_scales(width, name):
+            tile = sb_tile([P, width], U8, name)
+            nc.vector.memset(tile[:].bitcast(I32), 0)
+            return tile
+
+        def load_scales(tile, src, queue):
+            for q in range(4):
+                queue.dma_start(
+                    tile[32 * q : 32 * q + 4, :].bitcast(I32), src[0, 4 * q : 4 * q + 4, :].bitcast(I32)
+                )
+
+        def load_plane(t):
+            tile = sb_tile([P, T], F32, "ta%d" % t)
+            nc.sync.dma_start(tile[:], ta.rearrange("(p t) c -> p t c", t=PACK)[:, t, :])
+            return tile
+
+        def entries(lst, start, count):
+            return lst[:, start // LIST_ROWS : (start + count) // LIST_ROWS]
+
+        def fetch(dst, window, offsets, scale):
+            nc.scalar.activation(out=dst, in_=window[:].indirect(offsets), func=COPY, scale=scale)
+
+        def by_pairs(planes):
+            return planes.rearrange("p t (c i) -> p c t i", i=2)
+
+        def woven(tile):
+            return tile[:].rearrange("p (c i t) -> p c t i", i=2, t=PACK)
+
+        xo_sc = zeroed_scales(M, "xo_sc")
+        w2_sc_raw = zeroed_scales(R, "w2_sc_raw")
+        w_sc_raw = zeroed_scales(R, "w_sc_raw")
+        wb_sc = zeroed_scales(N, "wb_sc")
+        pages = []
+        for c in range(N // P):
+            page = sb_tile([P, E], F32, "page%d" % c)
+            nc.vector.memset(page[:], 0.0)
+            pages.append(page)
+
+        planes = [None] * PACK
+        l1 = load_list(offs, "l1")
+        ga_t = load_rowvec(ga, "ga_t")
+        planes[0] = load_plane(0)
+        l2 = load_list(offs2, "l2")
+        gb_t = load_rowvec(gb, "gb_t")
+        xo_w = sb_tile([P, M], U16, "xo_w")
+        nc.sync.dma_start(xo_w[:].bitcast(I32), xo_words[0].bitcast(I32))
+        l3 = load_list(offs3, "l3")
+        planes[2] = load_plane(2)
+        load_scales(xo_sc, xo_scales, nc.sync)
+        w2_raw = sb_tile([P, R], I32, "w2_raw")
+        nc.sync.dma_start(w2_raw[:], w2_words[0].rearrange("p n t -> p (n t)").bitcast(I32))
+        load_scales(w2_sc_raw, w2_scales, nc.gpsimd)
+        planes[3] = load_plane(3)
+        planes[1] = load_plane(1)
+        w_raw = sb_tile([P, 2 * R], U8, "w_raw")
+        nc.sync.dma_start(w_raw[:].bitcast(I32), w_words[0].bitcast(I32))
+        load_scales(w_sc_raw, w_scales, nc.gpsimd)
+        l5 = load_list(offs5, "l5")
+        sb_t = load_rowvec(sb, "sb_t")
+        l4 = load_list(offs4, "l4")
+        sa_t = load_rowvec(sa, "sa_t")
+        wb_w = sb_tile([P, N], I32, "wb_w")
+        nc.sync.dma_start(wb_w[:], wb_words[0].rearrange("p n t -> p (n t)").bitcast(I32))
+        load_scales(wb_sc, wb_scales, nc.sync)
+        so_t = sb_tile([P, N // P], F32, "so_t")
+        with nc.allow_non_contiguous_dma(reason="one value of so for each partition and tile"):
+            nc.sync.dma_start(so_t[:], so.rearrange("(c p) o -> p (c o)", p=P))
+        l6 = load_list(offs6, "l6")
+        l7 = load_list(offs7, "l7")
+
+        coarse = sb_tile([P, PACK, J], F32, "coarse")
+        fine = sb_tile([P, PACK, J], F32, "fine")
+
+        def fetch_codes(t, dst1, dst2, start, count):
+            fetch(dst1, planes[t], entries(l1, start, count), ga_t[:, t : t + 1])
+            fetch(dst2, planes[t], entries(l2, start, count), gb_t[:, t : t + 1])
+
+        fetch_codes(0, coarse[:, 0, :], fine[:, 0, :], 0, J)
+        for t in (2, 3):
+            fetch_codes(t, coarse[:, t, :JH], fine[:, t, :JH], 0, JH)
+        fetch_codes(1, coarse[:, 1, :JH], fine[:, 1, :JH], 0, JH)
+        fetch_codes(1, coarse[:, 1, JH:], fine[:, 1, JH:], JH, JH)
+        late = sb_tile([P, 2, 2, JH], F32, "late", tag="ta1")
+        for t in (2, 3):
+            fetch_codes(t, late[:, 0, t - 2, :], late[:, 1, t - 2, :], JH, JH)
+
+        xo_gw = sb_tile([P, J], U16, "xo_gw")
+        nc.vector.tensor_copy(xo_gw[:], xo_w[:].indirect(l3[:]))
+        xo_gs = sb_tile([P, J], U8, "xo_gs")
+        nc.vector.tensor_copy(xo_gs[:], xo_sc[:].indirect(l3[:]))
+        w2_w = sb_tile([P, R], I32, "w2_w")
+        nc.vector.tensor_copy(
+            w2_w[:].rearrange("p (t c i) -> p c t i", t=PACK, i=4),
+            w2_raw[:].rearrange("p (c i t) -> p c t i", t=PACK, i=4),
+        )
+        w2_sc = sb_tile([P, R], U8, "w2_sc")
+        nc.vector.tensor_copy(
+            w2_sc[:].rearrange("p (t m) -> p t m", t=PACK), w2_sc_raw[:].rearrange("p (m t) -> p t m", t=PACK)
+        )
+        w_w = sb_tile([P, 2 * R], U8, "w_w")
+        nc.vector.tensor_copy(
+            w_w[:].rearrange("p (t m b) -> p t m b", t=PACK, b=2),
+            w_raw[:].rearrange("p (m t b) -> p t m b", t=PACK, b=2),
+        )
+        w_sc = sb_tile([P, R], U8, "w_sc")
+        nc.vector.tensor_copy(
+            w_sc[:].rearrange("p (t m) -> p t m", t=PACK), w_sc_raw[:].rearrange("p (m t) -> p t m", t=PACK)
+        )
+
+        b_rows = []
+        for t in range(PACK):
+            bank = psum.tile([P, J], F32, name="b_ps%d" % t, tag="low%d" % t)
+            cols = slice(t * P, (t + 1) * P)
+            nc.tensor.matmul_mx(
+                out=bank[:], lhsT=w2_w[:, cols].bitcast(FP8X4), lhsT_scale=w2_sc[:, cols],
+                rhs=xo_gw[:].bitcast(FP4X4), rhs_scale=xo_gs[:], start=True, stop=True,
+            )
+            rows = sb_tile([P, J], F32, "b%d" % t)
+            nc.vector.tensor_copy(rows[:], bank[:])
+            b_rows.append(rows)
+
+        a_rows = [sb_tile([P, J], F32, "a%d" % t) for t in range(PACK)]
+        for h in range(2):
+            slots = slice(h * JH, (h + 1) * JH)
+            if h == 0:
+                xc = sb_tile([P, PACK * JH], BF16, "xc0")
+                nc.vector.tensor_tensor(woven(xc), by_pairs(coarse[:, :, slots]), by_pairs(fine[:, :, slots]), ADD)
+            else:
+                xc = sb_tile([P, PACK * JH], BF16, "xc1", tag="xc_w0")
+                nc.vector.tensor_tensor(
+                    woven(xc)[:, :, 0:2, :], by_pairs(coarse[:, 0:2, slots]), by_pairs(fine[:, 0:2, slots]), ADD
+                )
+                nc.vector.tensor_tensor(
+                    woven(xc)[:, :, 2:4, :], by_pairs(late[:, 0, :, :]), by_pairs(late[:, 1, :, :]), ADD
+                )
+            xc_w = sb_tile([P, JH], U32, "xc_w%d" % h)
+            xc_sc = sb_tile([P, JH], U8, "xc_sc%d" % h)
+            nc.vector.quantize_mx(out=xc_w[:].bitcast(FP8X4), scales=xc_sc[:], in_=xc[:])
+            for t in range(PACK):
+                bank = psum.tile([P, JH], F32, name="a_ps%d%d" % (h, t), tag=("low%d", "high%d")[h] % t)
+                nc.tensor.matmul_mx(
+                    out=bank[:], lhsT=w_w[:, 2 * t * P : 2 * (t + 1) * P].bitcast(FP4X4),
+                    lhsT_scale=w_sc[:, t * P : (t + 1) * P],
+                    rhs=xc_w[:].bitcast(FP8X4), rhs_scale=xc_sc[:], start=True, stop=True,
+                )
+                nc.vector.tensor_copy(a_rows[t][:, slots], bank[:])
+
+        second = sb_tile([P, PACK, O], F32, "second")
+        for t in range(PACK):
+            fetch(second[:, t, :], b_rows[t], l5[:], sb_t[:, t : t + 1])
+        p_rows = [sb_tile([P, O], F32, "p%d" % c) for c in range(N // P)]
+        firsts = []
+        for h in range(2):
+            first = sb_tile([P, PACK, OH], F32, "first%d" % h)
+            for t in range(PACK):
+                fetch(first[:, t, :], a_rows[t], entries(l4, h * OH, OH), sa_t[:, t : t + 1])
+            firsts.append(first)
+        for h in range(2):
+            places = slice(h * OH, (h + 1) * OH)
+            hid = sb_tile([P, PACK * OH], BF16, "hid%d" % h)
+            nc.vector.tensor_tensor(woven(hid), by_pairs(firsts[h][:]), by_pairs(second[:, :, places]), MAX)
+            hid_w = sb_tile([P, OH], U32, "hid_w%d" % h)
+            hid_sc = sb_tile([P, OH], U8, "hid_sc%d" % h)
+            nc.vector.quantize_mx(out=hid_w[:].bitcast(FP8X4), scales=hid_sc[:], in_=hid[:])
+            for c in range(N // P):
+                bank = psum.tile([P, OH], F32, name="p_ps%d%d" % (h, c), tag="low%d" % (2 * h + c))
+                cols = slice(c * P, (c + 1) * P)
+                nc.tensor.matmul_mx(
+                    out=bank[:], lhsT=wb_w[:, cols].bitcast(FP8X4), lhsT_scale=wb_sc[:, cols],
+                    rhs=hid_w[:].bitcast(FP8X4), rhs_scale=hid_sc[:], start=True, stop=True,
+                )
+                if h == 1 and c == 1:
+                    nc.vector.tensor_copy(p_rows[c][:, places], bank[:])
+                else:
+                    nc.scalar.copy(p_rows[c][:, places], bank[:])
+
+        for c in range(N // P):
+            ends = sb_tile([P, U], F32, "ends%d" % c)
+            fetch(ends[:], p_rows[c], l6[:], so_t[:, c : c + 1])
+            nc.vector.tensor_copy(pages[c][:].indirect(l7[:]), ends[:])
+            nc.sync.dma_start(out[c * P : (c + 1) * P, :], pages[c][:])

@@ -31,6 +31,7 @@ def tile_picked_refined_plain_two_groupmeet_one_posted_kernel(
     nc = tc.nc
     with ExitStack() as ctx:
         keep = ctx.enter_context(tc.tile_pool(name="keep", bufs=1))
+        shared = ctx.enter_context(tc.tile_pool(name="shared", bufs=1))
         psum = ctx.enter_context(tc.psum_pool(name="psum", bufs=1))
 
         def sb_tile(shape, dtype, name, tag=None):
@@ -51,10 +52,24 @@ def tile_picked_refined_plain_two_groupmeet_one_posted_kernel(
             nc.vector.memset(tile[:].bitcast(I32), 0)
             return tile
 
-        def load_scales(tile, src, queue):
-            for q in range(4):
-                queue.dma_start(
+        def load_scales(tile, src, quadrants):
+            for q in quadrants:
+                nc.sync.dma_start(
                     tile[32 * q : 32 * q + 4, :].bitcast(I32), src[0, 4 * q : 4 * q + 4, :].bitcast(I32)
+                )
+
+        def load_staged(tile, src):
+            for half in range(2):
+                nc.sync.dma_start(
+                    tile[64 * half : 64 * half + 4, :].bitcast(I32).rearrange("r (q n) -> r q n", q=2),
+                    src[0, 8 * half : 8 * half + 8, :].bitcast(I32).rearrange("(q r) n -> r q n", r=4),
+                )
+
+        def spread(tile):
+            for half in range(2):
+                nc.vector.tensor_copy(
+                    tile[64 * half + 32 : 64 * half + 36, :R].bitcast(I32),
+                    tile[64 * half : 64 * half + 4, R:].bitcast(I32),
                 )
 
         def load_plane(t):
@@ -74,9 +89,13 @@ def tile_picked_refined_plain_two_groupmeet_one_posted_kernel(
         def woven(tile):
             return tile[:].rearrange("p (c i t) -> p c t i", i=2, t=PACK)
 
+        warm_in = sb_tile([P, 8], F32, "warm_in")
+        nc.vector.memset(warm_in[:], 0.0)
         xo_sc = zeroed_scales(M, "xo_sc")
-        w2_sc_raw = zeroed_scales(R, "w2_sc_raw")
-        w_sc_raw = zeroed_scales(R, "w_sc_raw")
+        w2_sc_raw = sb_tile([P, 2 * R], U8, "w2_sc_raw")
+        nc.vector.memset(w2_sc_raw[:, :R].bitcast(I32), 0)
+        w_sc_raw = shared.tile([P, R], U8, name="w_sc_raw", align_bytes=64, offset=0)
+        nc.vector.memset(w_sc_raw[:, :R].bitcast(I32), 0)
         wb_sc = zeroed_scales(N, "wb_sc")
         pages = []
         for c in range(N // P):
@@ -84,75 +103,78 @@ def tile_picked_refined_plain_two_groupmeet_one_posted_kernel(
             nc.vector.memset(page[:], 0.0)
             pages.append(page)
 
+        warm_out = sb_tile([P, 8], F32, "warm_out")
+        nc.scalar.activation(out=warm_out[:], in_=warm_in[:], func=COPY)
         planes = [None] * PACK
+        planes[0] = load_plane(0)
         l1 = load_list(offs, "l1")
         ga_t = load_rowvec(ga, "ga_t")
-        planes[0] = load_plane(0)
-        l2 = load_list(offs2, "l2")
-        gb_t = load_rowvec(gb, "gb_t")
+        l3 = load_list(offs3, "l3")
         xo_w = sb_tile([P, M], U16, "xo_w")
         nc.sync.dma_start(xo_w[:].bitcast(I32), xo_words[0].bitcast(I32))
-        l3 = load_list(offs3, "l3")
-        planes[2] = load_plane(2)
-        load_scales(xo_sc, xo_scales, nc.sync)
+        l2 = load_list(offs2, "l2")
+        gb_t = load_rowvec(gb, "gb_t")
+        planes[1] = load_plane(1)
+        load_scales(xo_sc, xo_scales, range(4))
         w2_raw = sb_tile([P, R], I32, "w2_raw")
         nc.sync.dma_start(w2_raw[:], w2_words[0].rearrange("p n t -> p (n t)").bitcast(I32))
-        load_scales(w2_sc_raw, w2_scales, nc.gpsimd)
-        planes[3] = load_plane(3)
-        planes[1] = load_plane(1)
+        load_staged(w2_sc_raw, w2_scales)
         w_raw = sb_tile([P, 2 * R], U8, "w_raw")
         nc.sync.dma_start(w_raw[:].bitcast(I32), w_words[0].bitcast(I32))
-        load_scales(w_sc_raw, w_scales, nc.gpsimd)
+        planes[3] = load_plane(3)
+        load_scales(w_sc_raw, w_scales, range(4))
+        planes[2] = load_plane(2)
         l5 = load_list(offs5, "l5")
         sb_t = load_rowvec(sb, "sb_t")
         l4 = load_list(offs4, "l4")
         sa_t = load_rowvec(sa, "sa_t")
         wb_w = sb_tile([P, N], I32, "wb_w")
         nc.sync.dma_start(wb_w[:], wb_words[0].rearrange("p n t -> p (n t)").bitcast(I32))
-        load_scales(wb_sc, wb_scales, nc.sync)
+        load_scales(wb_sc, wb_scales, range(4))
         so_t = sb_tile([P, N // P], F32, "so_t")
         with nc.allow_non_contiguous_dma(reason="one value of so for each partition and tile"):
             nc.sync.dma_start(so_t[:], so.rearrange("(c p) o -> p (c o)", p=P))
         l6 = load_list(offs6, "l6")
         l7 = load_list(offs7, "l7")
 
-        coarse = sb_tile([P, PACK, J], F32, "coarse")
-        fine = sb_tile([P, PACK, J], F32, "fine")
+        early = sb_tile([P, 2, PACK, JH], F32, "early")
+        middle = sb_tile([P, 2, 3, JH], F32, "middle")
 
-        def fetch_codes(t, dst1, dst2, start, count):
-            fetch(dst1, planes[t], entries(l1, start, count), ga_t[:, t : t + 1])
-            fetch(dst2, planes[t], entries(l2, start, count), gb_t[:, t : t + 1])
+        def fetch_codes(t, dst, slot, start):
+            fetch(dst[:, 0, slot, :], planes[t], entries(l1, start, JH), ga_t[:, t : t + 1])
+            fetch(dst[:, 1, slot, :], planes[t], entries(l2, start, JH), gb_t[:, t : t + 1])
 
-        fetch_codes(0, coarse[:, 0, :], fine[:, 0, :], 0, J)
-        for t in (2, 3):
-            fetch_codes(t, coarse[:, t, :JH], fine[:, t, :JH], 0, JH)
-        fetch_codes(1, coarse[:, 1, :JH], fine[:, 1, :JH], 0, JH)
-        fetch_codes(1, coarse[:, 1, JH:], fine[:, 1, JH:], JH, JH)
-        late = sb_tile([P, 2, 2, JH], F32, "late", tag="ta1")
-        for t in (2, 3):
-            fetch_codes(t, late[:, 0, t - 2, :], late[:, 1, t - 2, :], JH, JH)
+        for t in (0, 1):
+            fetch_codes(t, early, t, 0)
+            fetch_codes(t, middle, t, JH)
+        for t in (3, 2):
+            fetch_codes(t, early, t, 0)
+        fetch_codes(2, middle, 2, JH)
+        late = sb_tile([P, 2, 1, JH], F32, "late", tag="ta2")
+        fetch_codes(3, late, 0, JH)
 
         xo_gw = sb_tile([P, J], U16, "xo_gw")
         nc.vector.tensor_copy(xo_gw[:], xo_w[:].indirect(l3[:]))
         xo_gs = sb_tile([P, J], U8, "xo_gs")
         nc.vector.tensor_copy(xo_gs[:], xo_sc[:].indirect(l3[:]))
+        spread(w2_sc_raw)
         w2_w = sb_tile([P, R], I32, "w2_w")
         nc.vector.tensor_copy(
             w2_w[:].rearrange("p (t c i) -> p c t i", t=PACK, i=4),
             w2_raw[:].rearrange("p (c i t) -> p c t i", t=PACK, i=4),
         )
-        w2_sc = sb_tile([P, R], U8, "w2_sc")
+        w2_sc = shared.tile([P, R], U8, name="w2_sc", align_bytes=64, offset=R)
         nc.vector.tensor_copy(
-            w2_sc[:].rearrange("p (t m) -> p t m", t=PACK), w2_sc_raw[:].rearrange("p (m t) -> p t m", t=PACK)
+            w2_sc[:].rearrange("p (t m) -> p t m", t=PACK), w2_sc_raw[:, :R].rearrange("p (m t) -> p t m", t=PACK)
         )
-        w_w = sb_tile([P, 2 * R], U8, "w_w")
+        w_w = sb_tile([P, 2 * R], U8, "w_w", tag="w2_sc_raw")
         nc.vector.tensor_copy(
             w_w[:].rearrange("p (t m b) -> p t m b", t=PACK, b=2),
             w_raw[:].rearrange("p (m t b) -> p t m b", t=PACK, b=2),
         )
         w_sc = sb_tile([P, R], U8, "w_sc")
         nc.vector.tensor_copy(
-            w_sc[:].rearrange("p (t m) -> p t m", t=PACK), w_sc_raw[:].rearrange("p (m t) -> p t m", t=PACK)
+            w_sc[:].rearrange("p (t m) -> p t m", t=PACK), w_sc_raw[:, :R].rearrange("p (m t) -> p t m", t=PACK)
         )
 
         b_rows = []
@@ -167,46 +189,55 @@ def tile_picked_refined_plain_two_groupmeet_one_posted_kernel(
             nc.vector.tensor_copy(rows[:], bank[:])
             b_rows.append(rows)
 
+        a_banks = [psum.tile([P, J], F32, name="a_ps%d" % t, tag="high%d" % t) for t in range(PACK)]
         a_rows = [sb_tile([P, J], F32, "a%d" % t) for t in range(PACK)]
         for h in range(2):
             slots = slice(h * JH, (h + 1) * JH)
             if h == 0:
-                xc = sb_tile([P, PACK * JH], BF16, "xc0")
-                nc.vector.tensor_tensor(woven(xc), by_pairs(coarse[:, :, slots]), by_pairs(fine[:, :, slots]), ADD)
+                xc = shared.tile([P, PACK * JH], BF16, name="xc0", align_bytes=64, offset=0)
+                nc.vector.tensor_tensor(woven(xc), by_pairs(early[:, 0, :, :]), by_pairs(early[:, 1, :, :]), ADD)
             else:
-                xc = sb_tile([P, PACK * JH], BF16, "xc1", tag="xc_w0")
-                nc.vector.tensor_tensor(
-                    woven(xc)[:, :, 0:2, :], by_pairs(coarse[:, 0:2, slots]), by_pairs(fine[:, 0:2, slots]), ADD
-                )
-                nc.vector.tensor_tensor(
-                    woven(xc)[:, :, 2:4, :], by_pairs(late[:, 0, :, :]), by_pairs(late[:, 1, :, :]), ADD
-                )
+                xc = shared.tile([P, PACK * JH], BF16, name="xc1", align_bytes=64, offset=0)
+                for part, src in ((slice(0, 3), middle), (slice(3, 4), late)):
+                    nc.vector.tensor_tensor(
+                        woven(xc)[:, :, part, :],
+                        by_pairs(src[:, 0, :, :]), by_pairs(src[:, 1, :, :]), ADD,
+                    )
             xc_w = sb_tile([P, JH], U32, "xc_w%d" % h)
             xc_sc = sb_tile([P, JH], U8, "xc_sc%d" % h)
             nc.vector.quantize_mx(out=xc_w[:].bitcast(FP8X4), scales=xc_sc[:], in_=xc[:])
             for t in range(PACK):
-                bank = psum.tile([P, JH], F32, name="a_ps%d%d" % (h, t), tag=("low%d", "high%d")[h] % t)
                 nc.tensor.matmul_mx(
-                    out=bank[:], lhsT=w_w[:, 2 * t * P : 2 * (t + 1) * P].bitcast(FP4X4),
+                    out=a_banks[t][:, slots], lhsT=w_w[:, 2 * t * P : 2 * (t + 1) * P].bitcast(FP4X4),
                     lhsT_scale=w_sc[:, t * P : (t + 1) * P],
                     rhs=xc_w[:].bitcast(FP8X4), rhs_scale=xc_sc[:], start=True, stop=True,
                 )
-                nc.vector.tensor_copy(a_rows[t][:, slots], bank[:])
+        for t in range(PACK):
+            nc.vector.tensor_copy(a_rows[t][:], a_banks[t][:])
 
-        second = sb_tile([P, PACK, O], F32, "second")
+        second = sb_tile([P, PACK, O], F32, "second", tag="ta3")
         for t in range(PACK):
             fetch(second[:, t, :], b_rows[t], l5[:], sb_t[:, t : t + 1])
         p_rows = [sb_tile([P, O], F32, "p%d" % c) for c in range(N // P)]
-        firsts = []
+        first_lo = sb_tile([P, 2, O], F32, "first_lo")
+        for t in (0, 1):
+            fetch(first_lo[:, t, :], a_rows[t], l4[:], sa_t[:, t : t + 1])
+        first_hi = [sb_tile([P, 2, OH], F32, "first_hi%d" % h) for h in range(2)]
         for h in range(2):
-            first = sb_tile([P, PACK, OH], F32, "first%d" % h)
-            for t in range(PACK):
-                fetch(first[:, t, :], a_rows[t], entries(l4, h * OH, OH), sa_t[:, t : t + 1])
-            firsts.append(first)
+            for t in (2, 3):
+                fetch(first_hi[h][:, t - 2, :], a_rows[t], entries(l4, h * OH, OH), sa_t[:, t : t + 1])
+        hids = [sb_tile([P, PACK * OH], BF16, "hid%d" % h) for h in range(2)]
         for h in range(2):
             places = slice(h * OH, (h + 1) * OH)
-            hid = sb_tile([P, PACK * OH], BF16, "hid%d" % h)
-            nc.vector.tensor_tensor(woven(hid), by_pairs(firsts[h][:]), by_pairs(second[:, :, places]), MAX)
+            nc.vector.tensor_tensor(
+                woven(hids[h])[:, :, 0:2, :], by_pairs(first_lo[:, :, places]), by_pairs(second[:, 0:2, places]), MAX
+            )
+        for h in range(2):
+            places = slice(h * OH, (h + 1) * OH)
+            hid = hids[h]
+            nc.vector.tensor_tensor(
+                woven(hid)[:, :, 2:4, :], by_pairs(first_hi[h][:]), by_pairs(second[:, 2:4, places]), MAX
+            )
             hid_w = sb_tile([P, OH], U32, "hid_w%d" % h)
             hid_sc = sb_tile([P, OH], U8, "hid_sc%d" % h)
             nc.vector.quantize_mx(out=hid_w[:].bitcast(FP8X4), scales=hid_sc[:], in_=hid[:])
@@ -217,7 +248,7 @@ def tile_picked_refined_plain_two_groupmeet_one_posted_kernel(
                     out=bank[:], lhsT=wb_w[:, cols].bitcast(FP8X4), lhsT_scale=wb_sc[:, cols],
                     rhs=hid_w[:].bitcast(FP8X4), rhs_scale=hid_sc[:], start=True, stop=True,
                 )
-                if h == 1 and c == 1:
+                if c == 1:
                     nc.vector.tensor_copy(p_rows[c][:, places], bank[:])
                 else:
                     nc.scalar.copy(p_rows[c][:, places], bank[:])

@@ -144,9 +144,11 @@ def tile_picked_refined_plain_two_groupmeet_one_posted_kernel(
             fetch(dst[:, 0, slot, :], planes[t], entries(l1, start, JH), ga_t[:, t : t + 1])
             fetch(dst[:, 1, slot, :], planes[t], entries(l2, start, JH), gb_t[:, t : t + 1])
 
-        for t in (0, 1):
-            fetch_codes(t, early, t, 0)
-            fetch_codes(t, middle, t, JH)
+        for lst, step, s in ((l1, ga_t, 0), (l2, gb_t, 1)):
+            fetch(early[:, s, 0, :], planes[0], entries(lst, 0, JH), step[:, 0:1])
+            fetch(middle[:, s, 0, :], planes[0], entries(lst, JH, JH), step[:, 0:1])
+        fetch_codes(1, early, 1, 0)
+        fetch_codes(1, middle, 1, JH)
         for t in (3, 2):
             fetch_codes(t, early, t, 0)
         fetch_codes(2, middle, 2, JH)
@@ -178,6 +180,7 @@ def tile_picked_refined_plain_two_groupmeet_one_posted_kernel(
         )
 
         b_rows = []
+        b_banks = []
         for t in range(PACK):
             bank = psum.tile([P, J], F32, name="b_ps%d" % t, tag="low%d" % t)
             cols = slice(t * P, (t + 1) * P)
@@ -185,9 +188,11 @@ def tile_picked_refined_plain_two_groupmeet_one_posted_kernel(
                 out=bank[:], lhsT=w2_w[:, cols].bitcast(FP8X4), lhsT_scale=w2_sc[:, cols],
                 rhs=xo_gw[:].bitcast(FP4X4), rhs_scale=xo_gs[:], start=True, stop=True,
             )
-            rows = sb_tile([P, J], F32, "b%d" % t)
-            nc.vector.tensor_copy(rows[:], bank[:])
-            b_rows.append(rows)
+            b_banks.append(bank)
+            if t < PACK - 1:
+                rows = sb_tile([P, J], F32, "b%d" % t)
+                nc.vector.tensor_copy(rows[:], bank[:])
+                b_rows.append(rows)
 
         a_banks = [psum.tile([P, J], F32, name="a_ps%d" % t, tag="high%d" % t) for t in range(PACK)]
         a_rows = [sb_tile([P, J], F32, "a%d" % t) for t in range(PACK)]
@@ -197,7 +202,7 @@ def tile_picked_refined_plain_two_groupmeet_one_posted_kernel(
                 xc = shared.tile([P, PACK * JH], BF16, name="xc0", align_bytes=64, offset=0)
                 nc.vector.tensor_tensor(woven(xc), by_pairs(early[:, 0, :, :]), by_pairs(early[:, 1, :, :]), ADD)
             else:
-                xc = shared.tile([P, PACK * JH], BF16, name="xc1", align_bytes=64, offset=0)
+                xc = sb_tile([P, PACK * JH], BF16, "xc1", tag="early")
                 for part, src in ((slice(0, 3), middle), (slice(3, 4), late)):
                     nc.vector.tensor_tensor(
                         woven(xc)[:, :, part, :],
@@ -212,6 +217,9 @@ def tile_picked_refined_plain_two_groupmeet_one_posted_kernel(
                     lhsT_scale=w_sc[:, t * P : (t + 1) * P],
                     rhs=xc_w[:].bitcast(FP8X4), rhs_scale=xc_sc[:], start=True, stop=True,
                 )
+        rows = sb_tile([P, J], F32, "b3", tag="early")
+        nc.vector.tensor_copy(rows[:], b_banks[3][:])
+        b_rows.append(rows)
         for t in range(PACK):
             nc.vector.tensor_copy(a_rows[t][:], a_banks[t][:])
 

from contextlib import ExitStack

import concourse.mybir as mybir

K, J, R, T, Z, M, O, N, U, E = 512, 512, 512, 1024, 512, 1024, 256, 256, 128, 512
FLOPS = 2 * (K * R * J + Z * R * J + R * N * O)

F32 = mybir.dt.float32
BF16 = mybir.dt.bfloat16
I32 = mybir.dt.int32
U32 = mybir.dt.uint32
U16 = mybir.dt.uint16
U8 = mybir.dt.uint8
FP8X4 = mybir.dt.float8_e4m3fn_x4
FP4X4 = mybir.dt.float4_e2m1fn_x4
COPY = mybir.ActivationFunctionType.Copy
ADD = mybir.AluOpType.add
MAX = mybir.AluOpType.max

P = 128
PACK = 4
LIST_ROWS = 16
JH = J // 2
OH = O // 2


def tile_picked_refined_plain_two_groupmeet_one_posted_kernel(
    tc, ta, ga, gb, w_words, w_scales, xo_words, xo_scales, w2_words, w2_scales, sa, sb,
    wb_words, wb_scales, so, offs, offs2, offs3, offs4, offs5, offs6, offs7, out,
):
    nc = tc.nc
    with ExitStack() as ctx:
        keep = ctx.enter_context(tc.tile_pool(name="keep", bufs=1))
        shared = ctx.enter_context(tc.tile_pool(name="shared", bufs=1))
        psum = ctx.enter_context(tc.psum_pool(name="psum", bufs=1))

        def sb_tile(shape, dtype, name, tag=None):
            return keep.tile(shape, dtype, name=name, tag=tag or name, align_bytes=64)

        def load_list(src, name):
            tile = sb_tile(list(src.shape), U16, name)
            nc.sync.dma_start(tile[:], src)
            return tile

        def load_rowvec(src, name):
            tile = sb_tile([P, PACK], F32, name)
            nc.sync.dma_start(tile[:], src.rearrange("(p t) o -> p (t o)", t=PACK))
            return tile

        def zeroed_scales(width, name):
            tile = sb_tile([P, width], U8, name)
            nc.vector.memset(tile[:].bitcast(I32), 0)
            return tile

        def load_scales(tile, src, quadrants):
            for q in quadrants:
                nc.sync.dma_start(
                    tile[32 * q : 32 * q + 4, :].bitcast(I32), src[0, 4 * q : 4 * q + 4, :].bitcast(I32)
                )

        def load_staged(tile, src):
            for half in range(2):
                nc.sync.dma_start(
                    tile[64 * half : 64 * half + 4, :].bitcast(I32).rearrange("r (q n) -> r q n", q=2),
                    src[0, 8 * half : 8 * half + 8, :].bitcast(I32).rearrange("(q r) n -> r q n", r=4),
                )

        def spread(tile):
            for half in range(2):
                nc.vector.tensor_copy(
                    tile[64 * half + 32 : 64 * half + 36, :R].bitcast(I32),
                    tile[64 * half : 64 * half + 4, R:].bitcast(I32),
                )

        def load_plane(t):
            tile = sb_tile([P, T], F32, "ta%d" % t)
            nc.sync.dma_start(tile[:], ta.rearrange("(p t) c -> p t c", t=PACK)[:, t, :])
            return tile

        def entries(lst, start, count):
            return lst[:, start // LIST_ROWS : (start + count) // LIST_ROWS]

        def fetch(dst, window, offsets, scale):
            nc.scalar.activation(out=dst, in_=window[:].indirect(offsets), func=COPY, scale=scale)

        def by_pairs(planes):
            return planes.rearrange("p t (c i) -> p c t i", i=2)

        def woven(tile):
            return tile[:].rearrange("p (c i t) -> p c t i", i=2, t=PACK)

        warm_in = sb_tile([P, 8], F32, "warm_in")
        nc.vector.memset(warm_in[:], 0.0)
        xo_sc = zeroed_scales(M, "xo_sc")
        w2_sc_raw = sb_tile([P, 2 * R], U8, "w2_sc_raw")
        nc.vector.memset(w2_sc_raw[:, :R].bitcast(I32), 0)
        w_sc_raw = shared.tile([P, R], U8, name="w_sc_raw", align_bytes=64, offset=0)
        nc.vector.memset(w_sc_raw[:, :R].bitcast(I32), 0)
        wb_sc = zeroed_scales(N, "wb_sc")
        pages = []
        for c in range(N // P):
            page = sb_tile([P, E], F32, "page%d" % c)
            nc.vector.memset(page[:], 0.0)
            pages.append(page)

        warm_out = sb_tile([P, 8], F32, "warm_out")
        nc.scalar.activation(out=warm_out[:], in_=warm_in[:], func=COPY)
        planes = [None] * PACK
        planes[0] = load_plane(0)
        l1 = load_list(offs, "l1")
        ga_t = load_rowvec(ga, "ga_t")
        l3 = load_list(offs3, "l3")
        xo_w = sb_tile([P, M], U16, "xo_w")
        nc.sync.dma_start(xo_w[:].bitcast(I32), xo_words[0].bitcast(I32))
        l2 = load_list(offs2, "l2")
        gb_t = load_rowvec(gb, "gb_t")
        planes[1] = load_plane(1)
        load_scales(xo_sc, xo_scales, range(4))
        w2_raw = sb_tile([P, R], I32, "w2_raw")
        nc.sync.dma_start(w2_raw[:], w2_words[0].rearrange("p n t -> p (n t)").bitcast(I32))
        load_staged(w2_sc_raw, w2_scales)
        w_raw = sb_tile([P, 2 * R], U8, "w_raw")
        nc.sync.dma_start(w_raw[:].bitcast(I32), w_words[0].bitcast(I32))
        planes[3] = load_plane(3)
        load_scales(w_sc_raw, w_scales, range(4))
        planes[2] = load_plane(2)
        l5 = load_list(offs5, "l5")
        sb_t = load_rowvec(sb, "sb_t")
        l4 = load_list(offs4, "l4")
        sa_t = load_rowvec(sa, "sa_t")
        wb_w = sb_tile([P, N], I32, "wb_w")
        nc.sync.dma_start(wb_w[:], wb_words[0].rearrange("p n t -> p (n t)").bitcast(I32))
        load_scales(wb_sc, wb_scales, range(4))
        so_t = sb_tile([P, N // P], F32, "so_t")
        with nc.allow_non_contiguous_dma(reason="one value of so for each partition and tile"):
            nc.sync.dma_start(so_t[:], so.rearrange("(c p) o -> p (c o)", p=P))
        l6 = load_list(offs6, "l6")
        l7 = load_list(offs7, "l7")

        early = sb_tile([P, 2, PACK, JH], F32, "early")
        middle = sb_tile([P, 2, 3, JH], F32, "middle")

        def fetch_codes(t, dst, slot, start):
            fetch(dst[:, 0, slot, :], planes[t], entries(l1, start, JH), ga_t[:, t : t + 1])
            fetch(dst[:, 1, slot, :], planes[t], entries(l2, start, JH), gb_t[:, t : t + 1])

        for lst, step, s in ((l1, ga_t, 0), (l2, gb_t, 1)):
            fetch(early[:, s, 0, :], planes[0], entries(lst, 0, JH), step[:, 0:1])
            fetch(middle[:, s, 0, :], planes[0], entries(lst, JH, JH), step[:, 0:1])
        fetch_codes(1, early, 1, 0)
        fetch_codes(1, middle, 1, JH)
        for t in (3, 2):
            fetch_codes(t, early, t, 0)
        fetch_codes(2, middle, 2, JH)
        late = sb_tile([P, 2, 1, JH], F32, "late", tag="ta2")
        fetch_codes(3, late, 0, JH)

        xo_gw = sb_tile([P, J], U16, "xo_gw")
        nc.vector.tensor_copy(xo_gw[:], xo_w[:].indirect(l3[:]))
        xo_gs = sb_tile([P, J], U8, "xo_gs")
        nc.vector.tensor_copy(xo_gs[:], xo_sc[:].indirect(l3[:]))
        spread(w2_sc_raw)
        w2_w = sb_tile([P, R], I32, "w2_w")
        nc.vector.tensor_copy(
            w2_w[:].rearrange("p (t c i) -> p c t i", t=PACK, i=4),
            w2_raw[:].rearrange("p (c i t) -> p c t i", t=PACK, i=4),
        )
        w2_sc = shared.tile([P, R], U8, name="w2_sc", align_bytes=64, offset=R)
        nc.vector.tensor_copy(
            w2_sc[:].rearrange("p (t m) -> p t m", t=PACK), w2_sc_raw[:, :R].rearrange("p (m t) -> p t m", t=PACK)
        )
        w_w = sb_tile([P, 2 * R], U8, "w_w", tag="w2_sc_raw")
        nc.vector.tensor_copy(
            w_w[:].rearrange("p (t m b) -> p t m b", t=PACK, b=2),
            w_raw[:].rearrange("p (m t b) -> p t m b", t=PACK, b=2),
        )
        w_sc = sb_tile([P, R], U8, "w_sc")
        nc.vector.tensor_copy(
            w_sc[:].rearrange("p (t m) -> p t m", t=PACK), w_sc_raw[:, :R].rearrange("p (m t) -> p t m", t=PACK)
        )

        b_rows = []
        b_banks = []
        for t in range(PACK):
            bank = psum.tile([P, J], F32, name="b_ps%d" % t, tag="low%d" % t)
            cols = slice(t * P, (t + 1) * P)
            nc.tensor.matmul_mx(
                out=bank[:], lhsT=w2_w[:, cols].bitcast(FP8X4), lhsT_scale=w2_sc[:, cols],
                rhs=xo_gw[:].bitcast(FP4X4), rhs_scale=xo_gs[:], start=True, stop=True,
            )
            b_banks.append(bank)
            if t < PACK - 1:
                rows = sb_tile([P, J], F32, "b%d" % t)
                nc.vector.tensor_copy(rows[:], bank[:])
                b_rows.append(rows)

        a_banks = [psum.tile([P, J], F32, name="a_ps%d" % t, tag="high%d" % t) for t in range(PACK)]
        a_rows = [sb_tile([P, J], F32, "a%d" % t) for t in range(PACK)]
        for h in range(2):
            slots = slice(h * JH, (h + 1) * JH)
            if h == 0:
                xc = shared.tile([P, PACK * JH], BF16, name="xc0", align_bytes=64, offset=0)
                nc.vector.tensor_tensor(woven(xc), by_pairs(early[:, 0, :, :]), by_pairs(early[:, 1, :, :]), ADD)
            else:
                xc = sb_tile([P, PACK * JH], BF16, "xc1", tag="early")
                for part, src in ((slice(0, 3), middle), (slice(3, 4), late)):
                    nc.vector.tensor_tensor(
                        woven(xc)[:, :, part, :],
                        by_pairs(src[:, 0, :, :]), by_pairs(src[:, 1, :, :]), ADD,
                    )
            xc_w = sb_tile([P, JH], U32, "xc_w%d" % h)
            xc_sc = sb_tile([P, JH], U8, "xc_sc%d" % h)
            nc.vector.quantize_mx(out=xc_w[:].bitcast(FP8X4), scales=xc_sc[:], in_=xc[:])
            for t in range(PACK):
                nc.tensor.matmul_mx(
                    out=a_banks[t][:, slots], lhsT=w_w[:, 2 * t * P : 2 * (t + 1) * P].bitcast(FP4X4),
                    lhsT_scale=w_sc[:, t * P : (t + 1) * P],
                    rhs=xc_w[:].bitcast(FP8X4), rhs_scale=xc_sc[:], start=True, stop=True,
                )
        rows = sb_tile([P, J], F32, "b3", tag="early")
        nc.vector.tensor_copy(rows[:], b_banks[3][:])
        b_rows.append(rows)
        for t in range(PACK):
            nc.vector.tensor_copy(a_rows[t][:], a_banks[t][:])

        second = sb_tile([P, PACK, O], F32, "second", tag="ta3")
        for t in range(PACK):
            fetch(second[:, t, :], b_rows[t], l5[:], sb_t[:, t : t + 1])
        p_rows = [sb_tile([P, O], F32, "p%d" % c) for c in range(N // P)]
        first_lo = sb_tile([P, 2, O], F32, "first_lo")
        for t in (0, 1):
            fetch(first_lo[:, t, :], a_rows[t], l4[:], sa_t[:, t : t + 1])
        first_hi = [sb_tile([P, 2, OH], F32, "first_hi%d" % h) for h in range(2)]
        for h in range(2):
            for t in (2, 3):
                fetch(first_hi[h][:, t - 2, :], a_rows[t], entries(l4, h * OH, OH), sa_t[:, t : t + 1])
        hids = [sb_tile([P, PACK * OH], BF16, "hid%d" % h) for h in range(2)]
        for h in range(2):
            places = slice(h * OH, (h + 1) * OH)
            nc.vector.tensor_tensor(
                woven(hids[h])[:, :, 0:2, :], by_pairs(first_lo[:, :, places]), by_pairs(second[:, 0:2, places]), MAX
            )
        for h in range(2):
            places = slice(h * OH, (h + 1) * OH)
            hid = hids[h]
            nc.vector.tensor_tensor(
                woven(hid)[:, :, 2:4, :], by_pairs(first_hi[h][:]), by_pairs(second[:, 2:4, places]), MAX
            )
            hid_w = sb_tile([P, OH], U32, "hid_w%d" % h)
            hid_sc = sb_tile([P, OH], U8, "hid_sc%d" % h)
            nc.vector.quantize_mx(out=hid_w[:].bitcast(FP8X4), scales=hid_sc[:], in_=hid[:])
            for c in range(N // P):
                bank = psum.tile([P, OH], F32, name="p_ps%d%d" % (h, c), tag="low%d" % (2 * h + c))
                cols = slice(c * P, (c + 1) * P)
                nc.tensor.matmul_mx(
                    out=bank[:], lhsT=wb_w[:, cols].bitcast(FP8X4), lhsT_scale=wb_sc[:, cols],
                    rhs=hid_w[:].bitcast(FP8X4), rhs_scale=hid_sc[:], start=True, stop=True,
                )
                if c == 1:
                    nc.vector.tensor_copy(p_rows[c][:, places], bank[:])
                else:
                    nc.scalar.copy(p_rows[c][:, places], bank[:])

        for c in range(N // P):
            ends = sb_tile([P, U], F32, "ends%d" % c)
            fetch(ends[:], p_rows[c], l6[:], so_t[:, c : c + 1])
            nc.vector.tensor_copy(pages[c][:].indirect(l7[:]), ends[:])
            nc.sync.dma_start(out[c * P : (c + 1) * P, :], pages[c][:])
